import numpy as np
import ml_dtypes


def mxq(x, axis, fmt="e4m3"):
    dtype, down = {"e4m3": (ml_dtypes.float8_e4m3fn, 7), "e5m2": (ml_dtypes.float8_e5m2, 14)}[fmt]
    v = np.moveaxis(np.asarray(x, np.float32).astype(ml_dtypes.bfloat16).astype(np.float64), axis, -1)
    blocks = v.reshape(v.shape[:-1] + (-1, 32))
    amax = np.abs(blocks).max(-1, keepdims=True)
    byte = np.maximum(np.where(amax > 0, np.frexp(amax)[1] - 1 + 127, 0) - down, 1)
    scale = np.exp2(byte - 127.0)
    codes = (blocks / scale).astype(np.float32).astype(dtype).astype(np.float64)
    return np.moveaxis((codes * scale).reshape(v.shape), -1, axis)


WIDE = False


def mx_kscale(k):
    if not WIDE:
        return np.ones(k)
    levels = np.array([30, -30])
    if k % 512:
        return np.exp2(np.random.permutation(np.resize(levels, k // 32))).repeat(32)
    a = np.empty((k // 512, 16))
    for p in range(k // 512):
        a[p, :8] = np.random.permutation(np.resize(levels, 8))
        for g in range(8):
            far = levels[np.abs(levels - a[p, g]) >= 10]
            a[p, g + 8] = far[np.random.randint(len(far))]
    return np.exp2(a.ravel()).repeat(32)


def f64(x):
    return np.asarray(x).astype(np.float64)


def striped(idx):
    return np.tile(np.asarray(idx).reshape(-1, 16).T, (8, 1)).astype(np.uint16)


def unstriped(offs):
    return offs[:16].T.reshape(-1).astype(np.int64)


E2M1 = np.array([0.0, 0.5, 1.0, 1.5, 2.0, 3.0, 4.0, 6.0, -0.0, -0.5, -1.0, -1.5, -2.0, -3.0, -4.0, -6.0])


def pack_weight(w, fmt):
    k, n = w.shape
    w = f64(np.asarray(w, np.float32).astype(ml_dtypes.bfloat16)).reshape(k // 32, 32, n)
    amax = np.abs(w).max(1)
    if fmt in ("e4m3", "e5m2"):
        byte = np.frexp(amax)[1] - 1 + 127 - (7 if fmt == "e4m3" else 14)
    else:
        mant, ex = np.frexp(amax / 6.0)
        byte = np.where(mant > 0.5, ex, ex - 1) + 127
    byte = np.clip(np.where(amax > 0, byte, 1), 1, 254)
    scaled = (w * np.exp2(127.0 - byte)[:, None, :]).reshape(k, n).astype(np.float32)
    by_word = np.ascontiguousarray(scaled.reshape(k // 512, 128, 4, n).transpose(0, 1, 3, 2))
    if fmt in ("e4m3", "e5m2"):
        words = by_word.astype(ml_dtypes.float8_e4m3fn if fmt == "e4m3" else ml_dtypes.float8_e5m2).view(np.uint8)
    else:
        c = by_word.astype(ml_dtypes.float4_e2m1fn).view(np.uint8) & 0xF
        words = (c[..., 0::2] | (c[..., 1::2] << 4)).reshape(k // 512, 128, 2 * n)
    return np.ascontiguousarray(words), np.ascontiguousarray(byte.astype(np.uint8).reshape(k // 512, 16, n))


def unpack_weight(words, scales, fmt):
    g, _, n = scales.shape
    words = np.ascontiguousarray(words).reshape(g, 128, n, -1)
    if fmt in ("e4m3", "e5m2"):
        vals = words.view(ml_dtypes.float8_e4m3fn if fmt == "e4m3" else ml_dtypes.float8_e5m2).astype(np.float64)
    else:
        nib = np.empty((g, 128, n, 4), np.uint8)
        nib[..., 0::2] = words & 0xF
        nib[..., 1::2] = words >> 4
        vals = E2M1[nib]
    vals = vals * np.repeat(np.exp2(scales.astype(np.float64) - 127.0), 8, axis=1)[..., None]
    return vals.transpose(0, 1, 3, 2).reshape(g * 512, n)


def bf(x):
    return np.asarray(x, np.float32).astype(ml_dtypes.bfloat16)


def planes(Y):
    r, m = Y.shape
    b = f64(bf(Y)).reshape(r // 32, 32, m)
    amax = np.abs(b).max(1)
    byte = np.clip(np.where(amax > 0, np.frexp(amax)[1] - 1 + 127 - 7, 1), 1, 254)
    codes = (b * np.exp2(127.0 - byte)[:, None, :]).reshape(r, m).astype(np.float32).astype(ml_dtypes.float8_e4m3fn).view(np.uint8)
    words = codes.reshape(r // 512, 128, 4, m).transpose(0, 1, 3, 2)
    return np.ascontiguousarray(words), np.ascontiguousarray(byte.astype(np.uint8).reshape(r // 512, 16, m))


K, T, Z, J, R, C, O, N, E = 512, 1024, 1024, 256, 512, 512, 256, 512, 1024


def setup_inputs():
    n = np.random.standard_normal
    idx = np.random.permutation(T)[:J]
    idx2 = np.random.permutation(Z)[:J]
    idx3 = np.random.permutation(C)[:J]
    idx4 = np.random.permutation(C)[:J]
    idx5 = np.random.permutation(C)[:O]
    idx6 = np.random.permutation(C)[:O]
    idx7 = np.random.permutation(E)[:O]
    fk = mx_kscale(K)
    fr = mx_kscale(R)
    xtp = pack_weight(n((K, T)) / fk[:, None], "e5m2")
    xop = pack_weight(n((K, Z)) / fk[:, None], "e4m3")
    wp = pack_weight(n((K, R)) * 1 / np.sqrt(K) * fk[:, None] * fr, "e2m1")
    wbp = pack_weight(n((R, N)) * 1 / np.sqrt(R) / fr[:, None], "e2m1")
    return {
        "xt_words": xtp[0],
        "xt_scales": xtp[1],
        "xo_words": xop[0],
        "xo_scales": xop[1],
        "w_words": wp[0],
        "w_scales": wp[1],
        "wb_words": wbp[0],
        "wb_scales": wbp[1],
        "tz": (n((N, E))).astype(np.float32),
        "offs": striped(idx),
        "offs2": striped(idx2),
        "offs3": striped(idx3),
        "offs4": striped(idx4),
        "offs5": striped(idx5),
        "offs6": striped(idx6),
        "offs7": striped(idx7),
    }


def reference(xt_words, xt_scales, xo_words, xo_scales, w_words, w_scales, wb_words, wb_scales, tz, offs, offs2, offs3, offs4, offs5, offs6, offs7):
    idx = unstriped(offs)
    idx2 = unstriped(offs2)
    idx3 = unstriped(offs3)
    idx4 = unstriped(offs4)
    idx5 = unstriped(offs5)
    idx6 = unstriped(offs6)
    idx7 = unstriped(offs7)
    xtu = unpack_weight(xt_words, xt_scales, "e5m2")
    xou = unpack_weight(xo_words, xo_scales, "e4m3")
    wu = unpack_weight(w_words, w_scales, "e2m1")
    wbu = unpack_weight(wb_words, wb_scales, "e2m1")
    xtidxg = xtu[:, idx]
    a = wu.T @ xtidxg
    xoidx2g = xou[:, idx2]
    b = wu.T @ xoidx2g
    pw = np.zeros((R, C))
    pw[:, idx3] = a
    pv = np.zeros((R, C))
    pv[:, idx4] = b
    hid = np.abs(pw[:, idx5] - pv[:, idx6])
    hidq = mxq(hid, 0, "e4m3")
    p = wbu.T @ hidq
    y = p + f64(tz)[:, idx7]
    words, scales = planes(y)
    return y, words, scales

@@ -1,0 +1,240 @@
+from contextlib import ExitStack
+
+import concourse.mybir as mybir
+
+K, T, Z, J, R, C, O, N, E = 512, 1024, 1024, 256, 512, 512, 256, 512, 1024
+FLOPS = 2 * K * R * J * 2 + 2 * R * N * O
+
+F32 = mybir.dt.float32
+BF16 = mybir.dt.bfloat16
+I32 = mybir.dt.int32
+U32 = mybir.dt.uint32
+U16 = mybir.dt.uint16
+U8 = mybir.dt.uint8
+E4M3 = mybir.dt.float8_e4m3fn_x4
+E5M2 = mybir.dt.float8_e5m2_x4
+E2M1 = mybir.dt.float4_e2m1fn_x4
+ACT = mybir.ActivationFunctionType
+ALU = mybir.AluOpType
+
+P = 128
+PACK = 4
+HALF = O // 2
+
+
+def tile_list_oneforboth_twoboards_one_tabled_pl_kernel(
+    tc, xt_words, xt_scales, xo_words, xo_scales, w_words, w_scales, wb_words, wb_scales, tz,
+    offs, offs2, offs3, offs4, offs5, offs6, offs7, out_0, out_1, out_2,
+):
+    nc = tc.nc
+    with ExitStack() as ctx:
+        lists = ctx.enter_context(tc.tile_pool(name="lists", bufs=1))
+        keep = ctx.enter_context(tc.tile_pool(name="keep", bufs=1))
+        psum = ctx.enter_context(tc.psum_pool(name="psum", bufs=1))
+
+        def load_list(src, name):
+            tile = lists.tile([P, 16], U16, name=name)
+            nc.sync.dma_start(tile[:], src)
+            return tile
+
+        def load_scales(queue, src, width, name):
+            tile = keep.tile([P, width], U8, name=name, align_bytes=64)
+            for q in range(4):
+                rows = src[0, 4 * q : 4 * q + 4, :].bitcast(I32)
+                queue.dma_start(out=tile[32 * q : 32 * q + 32, :].bitcast(I32), in_=rows.partition_broadcast(8))
+            return tile
+
+        def load_table_words(src, name):
+            tile = keep.tile([P, T], U32, name=name, align_bytes=64)
+            nc.sync.dma_start(out=tile[:].bitcast(I32), in_=src[0].rearrange("p n t -> p (n t)").bitcast(I32))
+            return tile
+
+        def load_weight_words(src, name):
+            tile = keep.tile([P, 2 * R], U8, name=name, align_bytes=64)
+            nc.sync.dma_start(out=tile[:].bitcast(I32), in_=src[0].bitcast(I32))
+            return tile
+
+        def deal_words(raw, name):
+            tile = keep.tile([P, 2 * R], U8, name=name, align_bytes=64)
+            nc.scalar.copy(
+                out=tile[:].bitcast(U16).rearrange("p (t m) -> p t m", t=PACK),
+                in_=raw[:].bitcast(U16).rearrange("p (m t) -> p t m", t=PACK),
+            )
+            return tile
+
+        def deal_scales(raw, name):
+            tile = keep.tile([P, R], U8, name=name, align_bytes=64)
+            nc.vector.tensor_copy(
+                out=tile[:].rearrange("p (t m) -> p t m", t=PACK),
+                in_=raw[:].rearrange("p (m t) -> p t m", t=PACK),
+            )
+            return tile
+
+        ws_raw = load_scales(nc.scalar, w_scales, R, "ws_raw")
+        l1 = load_list(offs, "l1")
+        xt_w = load_table_words(xt_words, "xt_w")
+        w_raw = load_weight_words(w_words, "w_raw")
+        xt_s = load_scales(nc.sync, xt_scales, T, "xt_s")
+        xo_w = load_table_words(xo_words, "xo_w")
+        l2 = load_list(offs2, "l2")
+        l3 = load_list(offs3, "l3")
+        xo_s = load_scales(nc.sync, xo_scales, Z, "xo_s")
+        l4 = load_list(offs4, "l4")
+        wb_raw = load_weight_words(wb_words, "wb_raw")
+        wbs_raw = load_scales(nc.sync, wb_scales, N, "wbs_raw")
+        l5 = load_list(offs5, "l5")
+        l6 = load_list(offs6, "l6")
+        l7 = load_list(offs7, "l7")
+        tz_rows = tz.rearrange("(p t) e -> p t e", t=PACK)
+        tz_sb = []
+        for t in range(PACK):
+            tile = keep.tile([P, E], F32, name=f"tz{t}")
+            nc.sync.dma_start(out=tile[:], in_=tz_rows[:, t, :])
+            tz_sb.append(tile)
+
+        boards = {}
+        for s in "ab":
+            for t in range(PACK):
+                tile = keep.tile([P, C], F32, name=f"board_{s}{t}")
+                nc.vector.memset(tile[:], 0.0)
+                boards[s, t] = tile
+
+        w_s = deal_scales(ws_raw, "w_s")
+        w_d = deal_words(w_raw, "w_d")
+
+        def gather_operand(words, scales, lst, name):
+            gw = keep.tile([P, J], U32, name=name + "_gw", align_bytes=64)
+            gs = keep.tile([P, J], U8, name=name + "_gs", align_bytes=64)
+            nc.vector.tensor_copy(gw[:], words[:].indirect(lst[:]))
+            nc.vector.tensor_copy(gs[:], scales[:].indirect(lst[:]))
+            return gw, gs
+
+        banks = {}
+
+        def first_products(s, gw, gs, fmt):
+            for t in range(PACK):
+                bank = psum.tile([P, J], F32, name=f"bank_{s}{t}", tag=f"bank{(0 if s == 'a' else 4) + t}")
+                nc.tensor.matmul_mx(
+                    out=bank[:],
+                    lhsT=w_d[:, 256 * t : 256 * (t + 1)].bitcast(E2M1),
+                    lhsT_scale=w_s[:, P * t : P * (t + 1)],
+                    rhs=gw[:].bitcast(fmt),
+                    rhs_scale=gs[:],
+                    start=True,
+                    stop=True,
+                )
+                banks[s, t] = bank
+
+        vals = {}
+
+        def fetch(s, t, on_scalar):
+            vals[s, t] = keep.tile([P, J], F32, name=f"vals_{s}{t}", tag=f"stage_{s}{t}")
+            if on_scalar:
+                nc.scalar.copy(vals[s, t][:], banks[s, t][:])
+            else:
+                nc.vector.tensor_copy(vals[s, t][:], banks[s, t][:])
+
+        def place(s, t, on_scalar):
+            lst = l3 if s == "a" else l4
+            if on_scalar:
+                nc.scalar.activation(boards[s, t][:].indirect(lst[:]), vals[s, t][:], ACT.Copy)
+            else:
+                nc.vector.tensor_copy(boards[s, t][:].indirect(lst[:]), vals[s, t][:])
+
+        a_w, a_s = gather_operand(xt_w, xt_s, l1, "xt")
+        first_products("a", a_w, a_s, E5M2)
+        b_w, b_s = gather_operand(xo_w, xo_s, l2, "xo")
+        first_products("b", b_w, b_s, E4M3)
+
+        for s in "ab":
+            for t in range(PACK):
+                fetch(s, t, t < 2)
+            for t in range(PACK):
+                place(s, t, t < 2)
+        wb_s = deal_scales(wbs_raw, "wb_s")
+        wb_d = deal_words(wb_raw, "wb_d")
+
+        diff = {}
+        tz_g = {}
+
+        def half(lst, h):
+            return lst[:, 8 * h : 8 * h + 8]
+
+        def look_boards(h):
+            pw_g = keep.tile([P, PACK, HALF], F32, name=f"pw_g{h}", tag=f"stage_b{h}")
+            diff[h] = keep.tile([P, PACK, HALF], F32, name=f"diff{h}", tag=f"diff{h}")
+            for t in range(PACK):
+                nc.scalar.activation(pw_g[:, t, :], boards["a", t][:].indirect(half(l5, h)), ACT.Copy)
+            for t in range(PACK):
+                nc.vector.tensor_tensor(
+                    diff[h][:, t, :], boards["b", t][:].indirect(half(l6, h)), pw_g[:, t, :], ALU.subtract
+                )
+
+        def look_tz(h):
+            tz_g[h] = keep.tile([P, PACK, HALF], F32, name=f"tz_g{h}", tag=("stage_b0", "diff0")[h])
+            for t in range(PACK):
+                window = tz_sb[t][:].indirect(half(l7, h))
+                if h == 0:
+                    nc.scalar.activation(tz_g[h][:, t, :], window, ACT.Copy)
+                else:
+                    nc.vector.tensor_copy(tz_g[h][:, t, :], window)
+
+        hid_codes = keep.tile([P, O], U32, name="hid_codes", align_bytes=64)
+        hid_scales = keep.tile([P, O], U8, name="hid_scales", align_bytes=64)
+        y_codes = keep.tile([P, O], U32, name="y_codes", align_bytes=64)
+        y_scales = keep.tile([P, O], U8, name="y_scales", align_bytes=64)
+        out_rows = out_0.rearrange("(p t) o -> p t o", t=PACK)
+        out_words = out_1[0].rearrange("p c t -> p (c t)").bitcast(I32)
+        y = {}
+
+        def second_stage(h):
+            cols = slice(HALF * h, HALF * (h + 1))
+            hid = keep.tile([P, HALF, PACK], BF16, name=f"hid{h}", align_bytes=64)
+            nc.scalar.activation(hid[:], diff[h][:].rearrange("p t o -> p o t"), ACT.Abs)
+            nc.vector.quantize_mx(
+                out=hid_codes[:, cols].bitcast(E4M3), scales=hid_scales[:, cols],
+                in_=hid[:].rearrange("p o t -> p (o t)"),
+            )
+            bank = psum.tile([P, PACK, HALF], F32, name=f"bank_p{h}", tag=f"bank{h}")
+            for t in range(PACK):
+                nc.tensor.matmul_mx(
+                    out=bank[:, t, :],
+                    lhsT=wb_d[:, 256 * t : 256 * (t + 1)].bitcast(E2M1),
+                    lhsT_scale=wb_s[:, P * t : P * (t + 1)],
+                    rhs=hid_codes[:, cols].bitcast(E4M3),
+                    rhs_scale=hid_scales[:, cols],
+                    start=True,
+                    stop=True,
+                )
+            y[h] = keep.tile([P, PACK, HALF], F32, name=f"y{h}")
+            return bank
+
+        def finish(h, bank):
+            cols = slice(HALF * h, HALF * (h + 1))
+            nc.vector.tensor_tensor(y[h][:], bank[:], tz_g[h][:], ALU.add)
+            nc.sync.dma_start(out=out_rows[:, :, cols], in_=y[h][:])
+            y_bf = keep.tile([P, HALF, PACK], BF16, name=f"y_bf{h}", align_bytes=64)
+            if h == 0:
+                nc.scalar.copy(y_bf[:], y[h][:].rearrange("p t o -> p o t"))
+            else:
+                nc.vector.tensor_copy(y_bf[:], y[h][:].rearrange("p t o -> p o t"))
+            nc.vector.quantize_mx(
+                out=y_codes[:, cols].bitcast(E4M3), scales=y_scales[:, cols],
+                in_=y_bf[:].rearrange("p o t -> p (o t)"),
+            )
+            nc.sync.dma_start(out=out_words[:, cols], in_=y_codes[:, cols].bitcast(I32))
+
+        look_boards(0)
+        look_boards(1)
+        bank0 = second_stage(0)
+        bank1 = second_stage(1)
+        look_tz(0)
+        look_tz(1)
+        finish(0, bank0)
+        finish(1, bank1)
+        for q in range(4):
+            queue = nc.sync if q % 2 == 0 else nc.scalar
+            queue.dma_start(
+                out=out_2[0, 4 * q : 4 * q + 4, :].bitcast(I32),
+                in_=y_scales[32 * q : 32 * q + 4, :].bitcast(I32),
+            )

@@ -37,26 +37,27 @@ def tile_list_oneforboth_twoboards_one_tabled_pl_kernel(
             nc.sync.dma_start(tile[:], src)
             return tile
 
-        def load_scales(queue, src, width, name):
-            tile = keep.tile([P, width], U8, name=name, align_bytes=64)
-            for q in range(4):
+        def scale_tile(width, name):
+            return keep.tile([P, width], U8, name=name, align_bytes=64)
+
+        def load_scales(queue, src, tile, quadrants=range(4)):
+            for q in quadrants:
                 rows = src[0, 4 * q : 4 * q + 4, :].bitcast(I32)
                 queue.dma_start(out=tile[32 * q : 32 * q + 32, :].bitcast(I32), in_=rows.partition_broadcast(8))
-            return tile
 
-        def load_table_words(src, name):
+        def load_table_words(queue, src, name):
             tile = keep.tile([P, T], U32, name=name, align_bytes=64)
-            nc.sync.dma_start(out=tile[:].bitcast(I32), in_=src[0].rearrange("p n t -> p (n t)").bitcast(I32))
+            queue.dma_start(out=tile[:].bitcast(I32), in_=src[0].rearrange("p n t -> p (n t)").bitcast(I32))
             return tile
 
-        def load_weight_words(src, name):
+        def load_weight_words(queue, src, name):
             tile = keep.tile([P, 2 * R], U8, name=name, align_bytes=64)
-            nc.sync.dma_start(out=tile[:].bitcast(I32), in_=src[0].bitcast(I32))
+            queue.dma_start(out=tile[:].bitcast(I32), in_=src[0].bitcast(I32))
             return tile
 
-        def deal_words(raw, name):
+        def deal_words(copy, raw, name):
             tile = keep.tile([P, 2 * R], U8, name=name, align_bytes=64)
-            nc.scalar.copy(
+            copy(
                 out=tile[:].bitcast(U16).rearrange("p (t m) -> p t m", t=PACK),
                 in_=raw[:].bitcast(U16).rearrange("p (m t) -> p t m", t=PACK),
             )
@@ -70,43 +71,52 @@ def tile_list_oneforboth_twoboards_one_tabled_pl_kernel(
             )
             return tile
 
-        ws_raw = load_scales(nc.scalar, w_scales, R, "ws_raw")
+        ws_raw = scale_tile(R, "ws_raw")
+        xt_s = scale_tile(T, "xt_s")
+        xo_s = scale_tile(Z, "xo_s")
+        wbs_raw = scale_tile(N, "wbs_raw")
+        tz_rows = tz.rearrange("(p t) e -> p t e", t=PACK)
+        tz_sb = [keep.tile([P, E], F32, name=f"tz{t}") for t in range(PACK)]
+
         l1 = load_list(offs, "l1")
-        xt_w = load_table_words(xt_words, "xt_w")
-        w_raw = load_weight_words(w_words, "w_raw")
-        xt_s = load_scales(nc.sync, xt_scales, T, "xt_s")
-        xo_w = load_table_words(xo_words, "xo_w")
+        load_scales(nc.scalar, xt_scales, xt_s, [2, 3])
+        load_scales(nc.scalar, w_scales, ws_raw, [0])
+        load_scales(nc.sync, xt_scales, xt_s, [0, 1])
+        w_raw = load_weight_words(nc.sync, w_words, "w_raw")
+        xt_w = load_table_words(nc.sync, xt_words, "xt_w")
+        load_scales(nc.sync, w_scales, ws_raw, [1, 2, 3])
         l2 = load_list(offs2, "l2")
         l3 = load_list(offs3, "l3")
-        xo_s = load_scales(nc.sync, xo_scales, Z, "xo_s")
+        xo_w = load_table_words(nc.sync, xo_words, "xo_w")
+        load_scales(nc.sync, xo_scales, xo_s)
+        load_scales(nc.sync, wb_scales, wbs_raw)
+        wb_raw = load_weight_words(nc.sync, wb_words, "wb_raw")
         l4 = load_list(offs4, "l4")
-        wb_raw = load_weight_words(wb_words, "wb_raw")
-        wbs_raw = load_scales(nc.sync, wb_scales, N, "wbs_raw")
         l5 = load_list(offs5, "l5")
-        l6 = load_list(offs6, "l6")
         l7 = load_list(offs7, "l7")
-        tz_rows = tz.rearrange("(p t) e -> p t e", t=PACK)
-        tz_sb = []
-        for t in range(PACK):
-            tile = keep.tile([P, E], F32, name=f"tz{t}")
-            nc.sync.dma_start(out=tile[:], in_=tz_rows[:, t, :])
-            tz_sb.append(tile)
+        for t in (0, 1, 3, 2):
+            if t == 3:
+                l6 = load_list(offs6, "l6")
+            nc.sync.dma_start(out=tz_sb[t][:], in_=tz_rows[:, t, :])
 
         boards = {}
-        for s in "ab":
-            for t in range(PACK):
+        for t in range(PACK):
+            for s in "ab":
                 tile = keep.tile([P, C], F32, name=f"board_{s}{t}")
-                nc.vector.memset(tile[:], 0.0)
+                engine = nc.vector if t < 2 else nc.gpsimd
+                engine.memset(tile[:].bitcast(I32), 0)
                 boards[s, t] = tile
 
-        w_s = deal_scales(ws_raw, "w_s")
-        w_d = deal_words(w_raw, "w_d")
+        w_d = deal_words(nc.scalar.copy, w_raw, "w_d")
 
         def gather_operand(words, scales, lst, name):
             gw = keep.tile([P, J], U32, name=name + "_gw", align_bytes=64)
             gs = keep.tile([P, J], U8, name=name + "_gs", align_bytes=64)
+            if name == "xt":
+                nc.vector.tensor_copy(gs[:], scales[:].indirect(lst[:]))
             nc.vector.tensor_copy(gw[:], words[:].indirect(lst[:]))
-            nc.vector.tensor_copy(gs[:], scales[:].indirect(lst[:]))
+            if name != "xt":
+                nc.vector.tensor_copy(gs[:], scales[:].indirect(lst[:]))
             return gw, gs
 
         banks = {}
@@ -117,7 +127,7 @@ def tile_list_oneforboth_twoboards_one_tabled_pl_kernel(
                 nc.tensor.matmul_mx(
                     out=bank[:],
                     lhsT=w_d[:, 256 * t : 256 * (t + 1)].bitcast(E2M1),
-                    lhsT_scale=w_s[:, P * t : P * (t + 1)],
+                    lhsT_scale=w_s[t][:],
                     rhs=gw[:].bitcast(fmt),
                     rhs_scale=gs[:],
                     start=True,
@@ -142,42 +152,54 @@ def tile_list_oneforboth_twoboards_one_tabled_pl_kernel(
                 nc.vector.tensor_copy(boards[s, t][:].indirect(lst[:]), vals[s, t][:])
 
         a_w, a_s = gather_operand(xt_w, xt_s, l1, "xt")
+        w_s = []
+        for t in range(PACK):
+            tile = keep.tile([P, P], U8, name=f"w_s{t}", align_bytes=64)
+            nc.vector.tensor_copy(out=tile[:], in_=ws_raw[:].rearrange("p (m t) -> p t m", t=PACK)[:, t, :])
+            w_s.append(tile)
         first_products("a", a_w, a_s, E5M2)
         b_w, b_s = gather_operand(xo_w, xo_s, l2, "xo")
         first_products("b", b_w, b_s, E4M3)
 
+        wb_s = deal_scales(wbs_raw, "wb_s")
+        wb_d = deal_words(nc.scalar.copy, wb_raw, "wb_d")
         for s in "ab":
             for t in range(PACK):
-                fetch(s, t, t < 2)
+                fetch(s, t, s == "a")
             for t in range(PACK):
-                place(s, t, t < 2)
-        wb_s = deal_scales(wbs_raw, "wb_s")
-        wb_d = deal_words(wb_raw, "wb_d")
+                place(s, t, s == "a")
 
         diff = {}
-        tz_g = {}
 
         def half(lst, h):
             return lst[:, 8 * h : 8 * h + 8]
 
+        pw_g = keep.tile([P, PACK, O], F32, name="pw_g", tag="stage_a2")
+        for t in range(PACK):
+            nc.scalar.activation(pw_g[:, t, :], boards["a", t][:].indirect(l5[:]), ACT.Copy)
+
         def look_boards(h):
-            pw_g = keep.tile([P, PACK, HALF], F32, name=f"pw_g{h}", tag=f"stage_b{h}")
             diff[h] = keep.tile([P, PACK, HALF], F32, name=f"diff{h}", tag=f"diff{h}")
             for t in range(PACK):
-                nc.scalar.activation(pw_g[:, t, :], boards["a", t][:].indirect(half(l5, h)), ACT.Copy)
-            for t in range(PACK):
                 nc.vector.tensor_tensor(
-                    diff[h][:, t, :], boards["b", t][:].indirect(half(l6, h)), pw_g[:, t, :], ALU.subtract
+                    diff[h][:, t, :], boards["b", t][:].indirect(half(l6, h)),
+                    pw_g[:, t, HALF * h : HALF * (h + 1)], ALU.subtract,
                 )
 
-        def look_tz(h):
-            tz_g[h] = keep.tile([P, PACK, HALF], F32, name=f"tz_g{h}", tag=("stage_b0", "diff0")[h])
-            for t in range(PACK):
-                window = tz_sb[t][:].indirect(half(l7, h))
-                if h == 0:
-                    nc.scalar.activation(tz_g[h][:, t, :], window, ACT.Copy)
-                else:
-                    nc.vector.tensor_copy(tz_g[h][:, t, :], window)
+        def woven(tile):
+            return tile[:].rearrange("p (c i) t -> p c t i", i=4)
+
+        def planes(tile):
+            return tile[:].rearrange("p t (c i) -> p c t i", i=4)
+
+        tz_g = keep.tile([P, PACK, O], F32, name="tz_g", tag="stage_a1")
+
+        def look_tz(t):
+            window = tz_sb[t][:].indirect(l7[:])
+            if t < PACK - 1:
+                nc.scalar.activation(tz_g[:, t, :], window, ACT.Copy)
+            else:
+                nc.vector.tensor_copy(tz_g[:, t, :], window)
 
         hid_codes = keep.tile([P, O], U32, name="hid_codes", align_bytes=64)
         hid_scales = keep.tile([P, O], U8, name="hid_scales", align_bytes=64)
@@ -190,46 +212,54 @@ def tile_list_oneforboth_twoboards_one_tabled_pl_kernel(
         def second_stage(h):
             cols = slice(HALF * h, HALF * (h + 1))
             hid = keep.tile([P, HALF, PACK], BF16, name=f"hid{h}", align_bytes=64)
-            nc.scalar.activation(hid[:], diff[h][:].rearrange("p t o -> p o t"), ACT.Abs)
+            nc.scalar.activation(woven(hid), planes(diff[h]), ACT.Abs)
             nc.vector.quantize_mx(
                 out=hid_codes[:, cols].bitcast(E4M3), scales=hid_scales[:, cols],
                 in_=hid[:].rearrange("p o t -> p (o t)"),
             )
-            bank = psum.tile([P, PACK, HALF], F32, name=f"bank_p{h}", tag=f"bank{h}")
-            for t in range(PACK):
-                nc.tensor.matmul_mx(
-                    out=bank[:, t, :],
-                    lhsT=wb_d[:, 256 * t : 256 * (t + 1)].bitcast(E2M1),
-                    lhsT_scale=wb_s[:, P * t : P * (t + 1)],
-                    rhs=hid_codes[:, cols].bitcast(E4M3),
-                    rhs_scale=hid_scales[:, cols],
-                    start=True,
-                    stop=True,
-                )
+            pair_banks = []
+            for u in range(2):
+                bank = psum.tile([P, 2, HALF], F32, name=f"bank_p{h}{u}", tag=f"bank{2 * h + u}")
+                for slot in range(2):
+                    t = 2 * u + slot
+                    nc.tensor.matmul_mx(
+                        out=bank[:, slot, :],
+                        lhsT=wb_d[:, 256 * t : 256 * (t + 1)].bitcast(E2M1),
+                        lhsT_scale=wb_s[:, P * t : P * (t + 1)],
+                        rhs=hid_codes[:, cols].bitcast(E4M3),
+                        rhs_scale=hid_scales[:, cols],
+                        start=True,
+                        stop=True,
+                    )
+                pair_banks.append(bank)
             y[h] = keep.tile([P, PACK, HALF], F32, name=f"y{h}")
-            return bank
+            return pair_banks
 
         def finish(h, bank):
             cols = slice(HALF * h, HALF * (h + 1))
-            nc.vector.tensor_tensor(y[h][:], bank[:], tz_g[h][:], ALU.add)
+            for u in range(2):
+                ts = slice(2 * u, 2 * u + 2)
+                nc.vector.tensor_tensor(y[h][:, ts, :], bank[u][:], tz_g[:, ts, cols], ALU.add)
             nc.sync.dma_start(out=out_rows[:, :, cols], in_=y[h][:])
             y_bf = keep.tile([P, HALF, PACK], BF16, name=f"y_bf{h}", align_bytes=64)
             if h == 0:
-                nc.scalar.copy(y_bf[:], y[h][:].rearrange("p t o -> p o t"))
+                nc.scalar.copy(woven(y_bf), planes(y[h]))
             else:
-                nc.vector.tensor_copy(y_bf[:], y[h][:].rearrange("p t o -> p o t"))
+                nc.vector.tensor_copy(woven(y_bf), planes(y[h]))
             nc.vector.quantize_mx(
                 out=y_codes[:, cols].bitcast(E4M3), scales=y_scales[:, cols],
                 in_=y_bf[:].rearrange("p o t -> p (o t)"),
             )
             nc.sync.dma_start(out=out_words[:, cols], in_=y_codes[:, cols].bitcast(I32))
 
+        look_tz(0)
+        look_tz(1)
         look_boards(0)
         look_boards(1)
         bank0 = second_stage(0)
+        look_tz(3)
         bank1 = second_stage(1)
-        look_tz(0)
-        look_tz(1)
+        look_tz(2)
         finish(0, bank0)
         finish(1, bank1)
         for q in range(4):

@@ -37,13 +37,19 @@ def tile_list_oneforboth_twoboards_one_tabled_pl_kernel(
             nc.sync.dma_start(tile[:], src)
             return tile
 
-        def scale_tile(width, name):
-            return keep.tile([P, width], U8, name=name, align_bytes=64)
+        def scale_tile(engine, width, name):
+            tile = keep.tile([P, width], U8, name=name, tag=name, align_bytes=64)
+            if engine is not None:
+                engine.memset(tile[:].bitcast(I32), 0)
+            return tile
 
-        def load_scales(queue, src, tile, quadrants=range(4)):
+        def load_scales(queue, src, tile, quadrants=range(4), spread=False):
             for q in quadrants:
                 rows = src[0, 4 * q : 4 * q + 4, :].bitcast(I32)
-                queue.dma_start(out=tile[32 * q : 32 * q + 32, :].bitcast(I32), in_=rows.partition_broadcast(8))
+                if spread:
+                    queue.dma_start(out=tile[32 * q : 32 * q + 32, :].bitcast(I32), in_=rows.partition_broadcast(8))
+                else:
+                    queue.dma_start(out=tile[32 * q : 32 * q + 4, :].bitcast(I32), in_=rows)
 
         def load_table_words(queue, src, name):
             tile = keep.tile([P, T], U32, name=name, align_bytes=64)
@@ -71,22 +77,21 @@ def tile_list_oneforboth_twoboards_one_tabled_pl_kernel(
             )
             return tile
 
-        ws_raw = scale_tile(R, "ws_raw")
-        xt_s = scale_tile(T, "xt_s")
-        xo_s = scale_tile(Z, "xo_s")
-        wbs_raw = scale_tile(N, "wbs_raw")
+        xt_s = scale_tile(None, T, "xt_s")
+        ws_raw = scale_tile(nc.vector, R, "ws_raw")
+        xo_s = scale_tile(nc.vector, Z, "xo_s")
+        wbs_raw = scale_tile(nc.gpsimd, N, "wbs_raw")
         tz_rows = tz.rearrange("(p t) e -> p t e", t=PACK)
         tz_sb = [keep.tile([P, E], F32, name=f"tz{t}") for t in range(PACK)]
 
         l1 = load_list(offs, "l1")
-        load_scales(nc.scalar, xt_scales, xt_s, [2, 3])
-        load_scales(nc.scalar, w_scales, ws_raw, [0])
-        load_scales(nc.sync, xt_scales, xt_s, [0, 1])
+        load_scales(nc.scalar, xt_scales, xt_s, [1, 2, 3], True)
+        load_scales(nc.sync, xt_scales, xt_s, [0], True)
+        l3 = load_list(offs3, "l3")
         w_raw = load_weight_words(nc.sync, w_words, "w_raw")
         xt_w = load_table_words(nc.sync, xt_words, "xt_w")
-        load_scales(nc.sync, w_scales, ws_raw, [1, 2, 3])
+        load_scales(nc.sync, w_scales, ws_raw)
         l2 = load_list(offs2, "l2")
-        l3 = load_list(offs3, "l3")
         xo_w = load_table_words(nc.sync, xo_words, "xo_w")
         load_scales(nc.sync, xo_scales, xo_s)
         load_scales(nc.sync, wb_scales, wbs_raw)
@@ -94,7 +99,7 @@ def tile_list_oneforboth_twoboards_one_tabled_pl_kernel(
         l4 = load_list(offs4, "l4")
         l5 = load_list(offs5, "l5")
         l7 = load_list(offs7, "l7")
-        for t in (0, 1, 3, 2):
+        for t in range(PACK):
             if t == 3:
                 l6 = load_list(offs6, "l6")
             nc.sync.dma_start(out=tz_sb[t][:], in_=tz_rows[:, t, :])
@@ -119,37 +124,41 @@ def tile_list_oneforboth_twoboards_one_tabled_pl_kernel(
                 nc.vector.tensor_copy(gs[:], scales[:].indirect(lst[:]))
             return gw, gs
 
+        groups = {"a": [(0,), (1, 2), (3,)], "b": [(0, 1), (2, 3)]}
         banks = {}
 
         def first_products(s, gw, gs, fmt):
-            for t in range(PACK):
-                bank = psum.tile([P, J], F32, name=f"bank_{s}{t}", tag=f"bank{(0 if s == 'a' else 4) + t}")
-                nc.tensor.matmul_mx(
-                    out=bank[:],
-                    lhsT=w_d[:, 256 * t : 256 * (t + 1)].bitcast(E2M1),
-                    lhsT_scale=w_s[t][:],
-                    rhs=gw[:].bitcast(fmt),
-                    rhs_scale=gs[:],
-                    start=True,
-                    stop=True,
-                )
-                banks[s, t] = bank
+            for group in groups[s]:
+                bank = psum.tile([P, len(group), J], F32, name=f"bank_{s}{group[0]}", tag=f"bank_{s}{group[0]}")
+                for slot, t in enumerate(group):
+                    nc.tensor.matmul_mx(
+                        out=bank[:, slot, :],
+                        lhsT=w_d[:, 256 * t : 256 * (t + 1)].bitcast(E2M1),
+                        lhsT_scale=w_s[t][:],
+                        rhs=gw[:].bitcast(fmt),
+                        rhs_scale=gs[:],
+                        start=True,
+                        stop=True,
+                    )
+                banks[s, group] = bank
 
         vals = {}
 
-        def fetch(s, t, on_scalar):
-            vals[s, t] = keep.tile([P, J], F32, name=f"vals_{s}{t}", tag=f"stage_{s}{t}")
+        def fetch(s, group, on_scalar, tag):
+            tile = keep.tile([P, len(group), J], F32, name=f"vals_{s}{group[0]}", tag=tag, align_bytes=64)
             if on_scalar:
-                nc.scalar.copy(vals[s, t][:], banks[s, t][:])
+                nc.scalar.copy(tile[:], banks[s, group][:])
             else:
-                nc.vector.tensor_copy(vals[s, t][:], banks[s, t][:])
+                nc.vector.tensor_copy(tile[:], banks[s, group][:])
+            for slot, t in enumerate(group):
+                vals[s, t] = tile[:, slot, :]
 
         def place(s, t, on_scalar):
             lst = l3 if s == "a" else l4
             if on_scalar:
-                nc.scalar.activation(boards[s, t][:].indirect(lst[:]), vals[s, t][:], ACT.Copy)
+                nc.scalar.activation(boards[s, t][:].indirect(lst[:]), vals[s, t], ACT.Copy)
             else:
-                nc.vector.tensor_copy(boards[s, t][:].indirect(lst[:]), vals[s, t][:])
+                nc.vector.tensor_copy(boards[s, t][:].indirect(lst[:]), vals[s, t])
 
         a_w, a_s = gather_operand(xt_w, xt_s, l1, "xt")
         w_s = []
@@ -161,20 +170,32 @@ def tile_list_oneforboth_twoboards_one_tabled_pl_kernel(
         b_w, b_s = gather_operand(xo_w, xo_s, l2, "xo")
         first_products("b", b_w, b_s, E4M3)
 
-        wb_s = deal_scales(wbs_raw, "wb_s")
-        wb_d = deal_words(nc.scalar.copy, wb_raw, "wb_d")
-        for s in "ab":
-            for t in range(PACK):
-                fetch(s, t, s == "a")
-            for t in range(PACK):
-                place(s, t, s == "a")
+        wb_s = keep.tile([P, N], U8, name="wb_s", align_bytes=64)
+        nc.gpsimd.tensor_copy(
+            out=wb_s[:].rearrange("p (t m) -> p t m", t=PACK),
+            in_=wbs_raw[:].rearrange("p (m t) -> p t m", t=PACK),
+        )
+        wb_d = keep.tile([P, 2 * N], U8, name="wb_d", align_bytes=64)
+        nc.gpsimd.tensor_copy(
+            out=wb_d[:].rearrange("p (t m b) -> p t m b", t=PACK, b=2),
+            in_=wb_raw[:].rearrange("p (m t b) -> p t m b", t=PACK, b=2),
+        )
+        fetch("a", (0,), True, "vals_a0")
+        fetch("a", (1, 2), True, "stage_a")
+        fetch("a", (3,), False, "xo_s")
+        for t in range(PACK):
+            place("a", t, t != 3)
+        fetch("b", (0, 1), False, "vals_b0")
+        fetch("b", (2, 3), False, "vals_b2")
+        for t in range(PACK):
+            place("b", t, t == 0)
 
         diff = {}
 
         def half(lst, h):
             return lst[:, 8 * h : 8 * h + 8]
 
-        pw_g = keep.tile([P, PACK, O], F32, name="pw_g", tag="stage_a2")
+        pw_g = keep.tile([P, PACK, O], F32, name="pw_g", tag="stage_a", align_bytes=64)
         for t in range(PACK):
             nc.scalar.activation(pw_g[:, t, :], boards["a", t][:].indirect(l5[:]), ACT.Copy)
 
@@ -192,7 +213,7 @@ def tile_list_oneforboth_twoboards_one_tabled_pl_kernel(
         def planes(tile):
             return tile[:].rearrange("p t (c i) -> p c t i", i=4)
 
-        tz_g = keep.tile([P, PACK, O], F32, name="tz_g", tag="stage_a1")
+        tz_g = keep.tile([P, PACK, O], F32, name="tz_g", tag="vals_a0", align_bytes=64)
 
         def look_tz(t):
             window = tz_sb[t][:].indirect(l7[:])
@@ -219,7 +240,7 @@ def tile_list_oneforboth_twoboards_one_tabled_pl_kernel(
             )
             pair_banks = []
             for u in range(2):
-                bank = psum.tile([P, 2, HALF], F32, name=f"bank_p{h}{u}", tag=f"bank{2 * h + u}")
+                bank = psum.tile([P, 2, HALF], F32, name=f"bank_p{h}{u}", tag=("bank_a0", "bank_a1", "bank_a3", "bank_b0")[2 * h + u])
                 for slot in range(2):
                     t = 2 * u + slot
                     nc.tensor.matmul_mx(
@@ -254,12 +275,12 @@ def tile_list_oneforboth_twoboards_one_tabled_pl_kernel(
 
         look_tz(0)
         look_tz(1)
+        look_tz(2)
         look_boards(0)
         look_boards(1)
         bank0 = second_stage(0)
         look_tz(3)
         bank1 = second_stage(1)
-        look_tz(2)
         finish(0, bank0)
         finish(1, bank1)
         for q in range(4):

from contextlib import ExitStack

import concourse.mybir as mybir

K, T, Z, J, R, C, O, N, E = 512, 1024, 1024, 256, 512, 512, 256, 512, 1024
FLOPS = 2 * K * R * J * 2 + 2 * R * N * O

F32 = mybir.dt.float32
BF16 = mybir.dt.bfloat16
I32 = mybir.dt.int32
U32 = mybir.dt.uint32
U16 = mybir.dt.uint16
U8 = mybir.dt.uint8
E4M3 = mybir.dt.float8_e4m3fn_x4
E5M2 = mybir.dt.float8_e5m2_x4
E2M1 = mybir.dt.float4_e2m1fn_x4
ACT = mybir.ActivationFunctionType
ALU = mybir.AluOpType

P = 128
PACK = 4
HALF = O // 2


def tile_list_oneforboth_twoboards_one_tabled_pl_kernel(
    tc, xt_words, xt_scales, xo_words, xo_scales, w_words, w_scales, wb_words, wb_scales, tz,
    offs, offs2, offs3, offs4, offs5, offs6, offs7, out_0, out_1, out_2,
):
    nc = tc.nc
    with ExitStack() as ctx:
        lists = ctx.enter_context(tc.tile_pool(name="lists", bufs=1))
        keep = ctx.enter_context(tc.tile_pool(name="keep", bufs=1))
        psum = ctx.enter_context(tc.psum_pool(name="psum", bufs=1))

        def load_list(src, name):
            tile = lists.tile([P, 16], U16, name=name)
            nc.sync.dma_start(tile[:], src)
            return tile

        def scale_tile(engine, width, name):
            tile = keep.tile([P, width], U8, name=name, tag=name, align_bytes=64)
            if engine is not None:
                engine.memset(tile[:].bitcast(I32), 0)
            return tile

        def load_scales(queue, src, tile, quadrants=range(4), spread=False):
            for q in quadrants:
                rows = src[0, 4 * q : 4 * q + 4, :].bitcast(I32)
                if spread:
                    queue.dma_start(out=tile[32 * q : 32 * q + 32, :].bitcast(I32), in_=rows.partition_broadcast(8))
                else:
                    queue.dma_start(out=tile[32 * q : 32 * q + 4, :].bitcast(I32), in_=rows)

        def load_table_words(queue, src, name):
            tile = keep.tile([P, T], U32, name=name, align_bytes=64)
            queue.dma_start(out=tile[:].bitcast(I32), in_=src[0].rearrange("p n t -> p (n t)").bitcast(I32))
            return tile

        def load_weight_words(queue, src, name):
            tile = keep.tile([P, 2 * R], U8, name=name, align_bytes=64)
            queue.dma_start(out=tile[:].bitcast(I32), in_=src[0].bitcast(I32))
            return tile

        def deal_words(copy, raw, name):
            tile = keep.tile([P, 2 * R], U8, name=name, align_bytes=64)
            copy(
                out=tile[:].bitcast(U16).rearrange("p (t m) -> p t m", t=PACK),
                in_=raw[:].bitcast(U16).rearrange("p (m t) -> p t m", t=PACK),
            )
            return tile

        def deal_scales(raw, name):
            tile = keep.tile([P, R], U8, name=name, align_bytes=64)
            nc.vector.tensor_copy(
                out=tile[:].rearrange("p (t m) -> p t m", t=PACK),
                in_=raw[:].rearrange("p (m t) -> p t m", t=PACK),
            )
            return tile

        xt_s = scale_tile(None, T, "xt_s")
        ws_raw = scale_tile(nc.vector, R, "ws_raw")
        xo_s = scale_tile(nc.vector, Z, "xo_s")
        wbs_raw = scale_tile(nc.gpsimd, N, "wbs_raw")
        tz_rows = tz.rearrange("(p t) e -> p t e", t=PACK)
        tz_sb = [keep.tile([P, E], F32, name=f"tz{t}") for t in range(PACK)]

        l1 = load_list(offs, "l1")
        load_scales(nc.scalar, xt_scales, xt_s, [1, 2, 3], True)
        load_scales(nc.sync, xt_scales, xt_s, [0], True)
        l3 = load_list(offs3, "l3")
        w_raw = load_weight_words(nc.sync, w_words, "w_raw")
        xt_w = load_table_words(nc.sync, xt_words, "xt_w")
        load_scales(nc.sync, w_scales, ws_raw)
        l2 = load_list(offs2, "l2")
        xo_w = load_table_words(nc.sync, xo_words, "xo_w")
        load_scales(nc.sync, xo_scales, xo_s)
        load_scales(nc.sync, wb_scales, wbs_raw)
        wb_raw = load_weight_words(nc.sync, wb_words, "wb_raw")
        l4 = load_list(offs4, "l4")
        l5 = load_list(offs5, "l5")
        l7 = load_list(offs7, "l7")
        for t in range(PACK):
            if t == 3:
                l6 = load_list(offs6, "l6")
            nc.sync.dma_start(out=tz_sb[t][:], in_=tz_rows[:, t, :])

        boards = {}
        for t in range(PACK):
            for s in "ab":
                tile = keep.tile([P, C], F32, name=f"board_{s}{t}")
                engine = nc.vector if t < 2 else nc.gpsimd
                engine.memset(tile[:].bitcast(I32), 0)
                boards[s, t] = tile

        w_d = deal_words(nc.scalar.copy, w_raw, "w_d")

        def gather_operand(words, scales, lst, name):
            gw = keep.tile([P, J], U32, name=name + "_gw", align_bytes=64)
            gs = keep.tile([P, J], U8, name=name + "_gs", align_bytes=64)
            if name == "xt":
                nc.vector.tensor_copy(gs[:], scales[:].indirect(lst[:]))
            nc.vector.tensor_copy(gw[:], words[:].indirect(lst[:]))
            if name != "xt":
                nc.vector.tensor_copy(gs[:], scales[:].indirect(lst[:]))
            return gw, gs

        groups = {"a": [(0,), (1, 2), (3,)], "b": [(0, 1), (2, 3)]}
        banks = {}

        def first_products(s, gw, gs, fmt):
            for group in groups[s]:
                bank = psum.tile([P, len(group), J], F32, name=f"bank_{s}{group[0]}", tag=f"bank_{s}{group[0]}")
                for slot, t in enumerate(group):
                    nc.tensor.matmul_mx(
                        out=bank[:, slot, :],
                        lhsT=w_d[:, 256 * t : 256 * (t + 1)].bitcast(E2M1),
                        lhsT_scale=w_s[t][:],
                        rhs=gw[:].bitcast(fmt),
                        rhs_scale=gs[:],
                        start=True,
                        stop=True,
                    )
                banks[s, group] = bank

        vals = {}

        def fetch(s, group, on_scalar, tag):
            tile = keep.tile([P, len(group), J], F32, name=f"vals_{s}{group[0]}", tag=tag, align_bytes=64)
            if on_scalar:
                nc.scalar.copy(tile[:], banks[s, group][:])
            else:
                nc.vector.tensor_copy(tile[:], banks[s, group][:])
            for slot, t in enumerate(group):
                vals[s, t] = tile[:, slot, :]

        def place(s, t, on_scalar):
            lst = l3 if s == "a" else l4
            if on_scalar:
                nc.scalar.activation(boards[s, t][:].indirect(lst[:]), vals[s, t], ACT.Copy)
            else:
                nc.vector.tensor_copy(boards[s, t][:].indirect(lst[:]), vals[s, t])

        a_w, a_s = gather_operand(xt_w, xt_s, l1, "xt")
        w_s = []
        for t in range(PACK):
            tile = keep.tile([P, P], U8, name=f"w_s{t}", align_bytes=64)
            nc.vector.tensor_copy(out=tile[:], in_=ws_raw[:].rearrange("p (m t) -> p t m", t=PACK)[:, t, :])
            w_s.append(tile)
        first_products("a", a_w, a_s, E5M2)
        b_w, b_s = gather_operand(xo_w, xo_s, l2, "xo")
        first_products("b", b_w, b_s, E4M3)

        wb_s = keep.tile([P, N], U8, name="wb_s", align_bytes=64)
        nc.gpsimd.tensor_copy(
            out=wb_s[:].rearrange("p (t m) -> p t m", t=PACK),
            in_=wbs_raw[:].rearrange("p (m t) -> p t m", t=PACK),
        )
        wb_d = keep.tile([P, 2 * N], U8, name="wb_d", align_bytes=64)
        nc.gpsimd.tensor_copy(
            out=wb_d[:].rearrange("p (t m b) -> p t m b", t=PACK, b=2),
            in_=wb_raw[:].rearrange("p (m t b) -> p t m b", t=PACK, b=2),
        )
        fetch("a", (0,), True, "vals_a0")
        fetch("a", (1, 2), True, "stage_a")
        fetch("a", (3,), False, "xo_s")
        for t in range(PACK):
            place("a", t, t != 3)
        fetch("b", (0, 1), False, "vals_b0")
        fetch("b", (2, 3), False, "vals_b2")
        for t in range(PACK):
            place("b", t, t == 0)

        diff = {}

        def half(lst, h):
            return lst[:, 8 * h : 8 * h + 8]

        pw_g = keep.tile([P, PACK, O], F32, name="pw_g", tag="stage_a", align_bytes=64)
        for t in range(PACK):
            nc.scalar.activation(pw_g[:, t, :], boards["a", t][:].indirect(l5[:]), ACT.Copy)

        def look_boards(h):
            diff[h] = keep.tile([P, PACK, HALF], F32, name=f"diff{h}", tag=f"diff{h}")
            for t in range(PACK):
                nc.vector.tensor_tensor(
                    diff[h][:, t, :], boards["b", t][:].indirect(half(l6, h)),
                    pw_g[:, t, HALF * h : HALF * (h + 1)], ALU.subtract,
                )

        def woven(tile):
            return tile[:].rearrange("p (c i) t -> p c t i", i=4)

        def planes(tile):
            return tile[:].rearrange("p t (c i) -> p c t i", i=4)

        tz_g = keep.tile([P, PACK, O], F32, name="tz_g", tag="vals_a0", align_bytes=64)

        def look_tz(t):
            window = tz_sb[t][:].indirect(l7[:])
            if t < PACK - 1:
                nc.scalar.activation(tz_g[:, t, :], window, ACT.Copy)
            else:
                nc.vector.tensor_copy(tz_g[:, t, :], window)

        hid_codes = keep.tile([P, O], U32, name="hid_codes", align_bytes=64)
        hid_scales = keep.tile([P, O], U8, name="hid_scales", align_bytes=64)
        y_codes = keep.tile([P, O], U32, name="y_codes", align_bytes=64)
        y_scales = keep.tile([P, O], U8, name="y_scales", align_bytes=64)
        out_rows = out_0.rearrange("(p t) o -> p t o", t=PACK)
        out_words = out_1[0].rearrange("p c t -> p (c t)").bitcast(I32)
        y = {}

        def second_stage(h):
            cols = slice(HALF * h, HALF * (h + 1))
            hid = keep.tile([P, HALF, PACK], BF16, name=f"hid{h}", align_bytes=64)
            nc.scalar.activation(woven(hid), planes(diff[h]), ACT.Abs)
            nc.vector.quantize_mx(
                out=hid_codes[:, cols].bitcast(E4M3), scales=hid_scales[:, cols],
                in_=hid[:].rearrange("p o t -> p (o t)"),
            )
            pair_banks = []
            for u in range(2):
                bank = psum.tile([P, 2, HALF], F32, name=f"bank_p{h}{u}", tag=("bank_a0", "bank_a1", "bank_a3", "bank_b0")[2 * h + u])
                for slot in range(2):
                    t = 2 * u + slot
                    nc.tensor.matmul_mx(
                        out=bank[:, slot, :],
                        lhsT=wb_d[:, 256 * t : 256 * (t + 1)].bitcast(E2M1),
                        lhsT_scale=wb_s[:, P * t : P * (t + 1)],
                        rhs=hid_codes[:, cols].bitcast(E4M3),
                        rhs_scale=hid_scales[:, cols],
                        start=True,
                        stop=True,
                    )
                pair_banks.append(bank)
            y[h] = keep.tile([P, PACK, HALF], F32, name=f"y{h}")
            return pair_banks

        def finish(h, bank):
            cols = slice(HALF * h, HALF * (h + 1))
            for u in range(2):
                ts = slice(2 * u, 2 * u + 2)
                nc.vector.tensor_tensor(y[h][:, ts, :], bank[u][:], tz_g[:, ts, cols], ALU.add)
            nc.sync.dma_start(out=out_rows[:, :, cols], in_=y[h][:])
            y_bf = keep.tile([P, HALF, PACK], BF16, name=f"y_bf{h}", align_bytes=64)
            if h == 0:
                nc.scalar.copy(woven(y_bf), planes(y[h]))
            else:
                nc.vector.tensor_copy(woven(y_bf), planes(y[h]))
            nc.vector.quantize_mx(
                out=y_codes[:, cols].bitcast(E4M3), scales=y_scales[:, cols],
                in_=y_bf[:].rearrange("p o t -> p (o t)"),
            )
            nc.sync.dma_start(out=out_words[:, cols], in_=y_codes[:, cols].bitcast(I32))

        look_tz(0)
        look_tz(1)
        look_tz(2)
        look_boards(0)
        look_boards(1)
        bank0 = second_stage(0)
        look_tz(3)
        bank1 = second_stage(1)
        finish(0, bank0)
        finish(1, bank1)
        for q in range(4):
            queue = nc.sync if q % 2 == 0 else nc.scalar
            queue.dma_start(
                out=out_2[0, 4 * q : 4 * q + 4, :].bitcast(I32),
                in_=y_scales[32 * q : 32 * q + 4, :].bitcast(I32),
            )
